import numpy as np
import ml_dtypes


def mxq(x, axis, fmt="e4m3"):
    dtype, down = {"e4m3": (ml_dtypes.float8_e4m3fn, 7), "e5m2": (ml_dtypes.float8_e5m2, 14)}[fmt]
    v = np.moveaxis(np.asarray(x, np.float32).astype(ml_dtypes.bfloat16).astype(np.float64), axis, -1)
    blocks = v.reshape(v.shape[:-1] + (-1, 32))
    amax = np.abs(blocks).max(-1, keepdims=True)
    byte = np.maximum(np.where(amax > 0, np.frexp(amax)[1] - 1 + 127, 0) - down, 1)
    scale = np.exp2(byte - 127.0)
    codes = (blocks / scale).astype(np.float32).astype(dtype).astype(np.float64)
    return np.moveaxis((codes * scale).reshape(v.shape), -1, axis)


WIDE = False


def mx_kscale(k):
    if not WIDE:
        return np.ones(k)
    levels = np.array([10, -10, 5, -5, 0])
    if k % 512:
        return np.exp2(np.random.permutation(np.resize(levels, k // 32))).repeat(32)
    a = np.empty((k // 512, 16))
    for p in range(k // 512):
        a[p, :8] = np.random.permutation(np.resize(levels, 8))
        for g in range(8):
            far = levels[np.abs(levels - a[p, g]) >= 10]
            a[p, g + 8] = far[np.random.randint(len(far))]
    return np.exp2(a.ravel()).repeat(32)


def f64(x):
    return np.asarray(x).astype(np.float64)


def striped(idx):
    return np.tile(idx.reshape(-1, 16).T, (8, 1)).astype(np.uint16)


def unstriped(offs):
    return offs[:16].T.reshape(-1).astype(np.int64)


def pack_weight(w):
    k, n = w.shape
    w = f64(np.asarray(w, np.float32).astype(ml_dtypes.bfloat16)).reshape(k // 32, 32, n)
    amax = np.abs(w).max(1)
    byte = np.clip(np.where(amax > 0, np.frexp(amax)[1] - 1 + 127 - 7, 1), 1, 254)
    scaled = (w * np.exp2(127.0 - byte)[:, None, :]).reshape(k, n).astype(np.float32)
    words = np.ascontiguousarray(scaled.reshape(k // 512, 128, 4, n).transpose(0, 1, 3, 2)).astype(ml_dtypes.float8_e4m3fn).view(np.uint8)
    return words, np.ascontiguousarray(byte.astype(np.uint8).reshape(k // 512, 16, n))


def unpack_weight(words, scales):
    g, p, n, _ = words.shape
    vals = np.ascontiguousarray(words).view(ml_dtypes.float8_e4m3fn).astype(np.float64) * np.repeat(np.exp2(scales.astype(np.float64) - 127.0), 8, axis=1)[..., None]
    return vals.transpose(0, 1, 3, 2).reshape(g * 512, n)


K, T, S, D, N, V = 512, 2048, 512, 2, 128, 256
P = 2 ** 7


def setup_inputs():
    n = np.random.standard_normal
    s = mx_kscale(K)[:, None]
    packed_xT = pack_weight(n((K, T)) * s)
    return {
        "x_words": packed_xT[0],
        "x_scales": packed_xT[1],
        "w1": (n((K, N)) / np.sqrt(K) / s).astype(np.float32),
        "w2": (n((K, N)) / np.sqrt(K) / s).astype(np.float32),
        "dose": (np.tile(np.random.uniform(0.2, 1.0, S), (P, 1))).astype(np.float32),
        "gf0": (-np.random.uniform(0.5, 2.0, (N, 1))).astype(np.float32),
        "gb0": (-np.random.uniform(0.2, 1.5, (N, 1))).astype(np.float32),
        "amp": (np.tile(np.random.uniform(0.5, 1.5, V), (P, 1))).astype(np.float32),
        "offs": striped(np.random.permutation(T)[:S]),
    }


def reference(x_words, x_scales, w1, w2, dose, gf0, gb0, amp, offs):
    xq = unpack_weight(x_words, x_scales)[:, unstriped(offs)]
    y2 = ((mxq(f64(w2), 0, "e4m3").T @ xq)) * f64(dose)[:1]
    gb = y2.reshape(len(y2), -1, D).mean(axis=2) + f64(gb0)
    y1 = ((mxq(f64(w1), 0, "e4m3").T @ xq)) * f64(dose)[:1]
    gf = y1.reshape(len(y1), -1, D).mean(axis=2) + f64(gf0)
    ef = np.exp(gf)
    return f64(amp)[:1] / (np.exp(gb) * (ef + 1.0) + 1.0)

@@ -1,0 +1,129 @@
+from contextlib import ExitStack
+
+import concourse.mybir as mybir
+from concourse.masks import make_identity
+
+K, T, S, D, N, V = 512, 2048, 512, 2, 128, 256
+FLOPS = 2 * 2 * K * N * S
+
+F32 = mybir.dt.float32
+BF16 = mybir.dt.bfloat16
+I32 = mybir.dt.int32
+U32 = mybir.dt.uint32
+U16 = mybir.dt.uint16
+U8 = mybir.dt.uint8
+FP8X4 = mybir.dt.float8_e4m3fn_x4
+ADD = mybir.AluOpType.add
+MULT = mybir.AluOpType.mult
+EXP = mybir.ActivationFunctionType.Exp
+
+P = 128
+PACK = 4
+HALVES = 2
+HS = S // HALVES
+HV = V // HALVES
+
+
+def tile_picked_ythermo_bind_p_kernel(tc, x_words, x_scales, w1, w2, dose, gf0, gb0, amp, offs, out):
+    nc = tc.nc
+    with ExitStack() as ctx:
+        pool = ctx.enter_context(tc.tile_pool(name="pool", bufs=1))
+        psum = ctx.enter_context(tc.psum_pool(name="psum", bufs=1))
+
+        offsets = pool.tile([P, S // 16], U16, name="offsets")
+        scale_table = pool.tile([P, T], U8, name="scale_table", align_bytes=64)
+        word_table = pool.tile([P, T], I32, name="word_table", align_bytes=64)
+        w_raw = [pool.tile([P, PACK, N], F32, name="w_raw%d" % i, align_bytes=64) for i in range(2)]
+
+        nc.vector.memset(scale_table[:].bitcast(I32), 0)
+        nc.sync.dma_start(w_raw[0][:], w1.rearrange("(p j) n -> p j n", j=PACK))
+        nc.sync.dma_start(offsets[:], offs)
+        for q in range(4):
+            nc.sync.dma_start(scale_table[32 * q : 32 * q + 4, :].bitcast(I32), x_scales[0, 4 * q : 4 * q + 4, :].bitcast(I32))
+        nc.sync.dma_start(word_table[:], x_words[0].rearrange("p n t -> p (n t)").bitcast(I32))
+        nc.sync.dma_start(w_raw[1][:], w2.rearrange("(p j) n -> p j n", j=PACK))
+
+        bias = [pool.tile([P, 1], F32, name="bias%d" % i) for i in range(2)]
+        nc.sync.dma_start(bias[0][:], gf0)
+        nc.sync.dma_start(bias[1][:], gb0)
+
+        dose_cols = pool.tile([P, 4], F32, name="dose_cols")
+        amp_cols = pool.tile([P, 2], F32, name="amp_cols")
+        nc.gpsimd.dma_start(dose_cols[:], dose[0].rearrange("(p c) -> p c", c=4))
+        nc.gpsimd.dma_start(amp_cols[:], amp[0].rearrange("(p c) -> p c", c=2))
+        identity = pool.tile([P, P], F32, name="identity")
+        make_identity(nc, identity[:])
+
+        inv_amp_cols = pool.tile([P, 2], F32, name="inv_amp_cols")
+        nc.vector.reciprocal(inv_amp_cols[:], amp_cols[:])
+        dose_bank = psum.tile([P, 4, P], F32, name="dose_bank")
+        inv_amp_bank = psum.tile([P, 2, P], F32, name="inv_amp_bank")
+        for c in range(4):
+            nc.tensor.transpose(dose_bank[:, c, :], dose_cols[:, c : c + 1].to_broadcast([P, P]), identity[:])
+        for c in range(2):
+            nc.tensor.transpose(inv_amp_bank[:, c, :], inv_amp_cols[:, c : c + 1].to_broadcast([P, P]), identity[:])
+        dose_rows = pool.tile([P, HALVES, D, HV], F32, name="dose_rows")
+        nc.scalar.copy(
+            dose_rows[:].rearrange("q h d (w e) -> q h d w e", e=2),
+            dose_bank[:].rearrange("q (e d) (h w) -> q h d w e", d=D, h=HALVES),
+        )
+
+        w_codes = [pool.tile([P, N], U32, name="w_codes%d" % i, align_bytes=64) for i in range(2)]
+        w_scales = [pool.tile([P, N], U8, name="w_scales%d" % i, align_bytes=64) for i in range(2)]
+        w_grouped = [pool.tile([P, N, PACK], BF16, name="w_grouped%d" % i, align_bytes=64) for i in range(2)]
+
+        def grouped_view(i):
+            return w_grouped[i][:].rearrange("p (c e) j -> p c j e", e=4)
+
+        def raw_view(i):
+            return w_raw[i][:].rearrange("p j (c e) -> p c j e", e=4)
+
+        def quantize(i):
+            nc.vector.quantize_mx(out=w_codes[i][:].bitcast(FP8X4), scales=w_scales[i][:], in_=w_grouped[i][:].rearrange("p n j -> p (n j)"))
+
+        nc.vector.tensor_copy(grouped_view(0), raw_view(0))
+        quantize(0)
+
+        picked_scales = pool.tile([P, S], U8, name="picked_scales", align_bytes=64)
+        nc.vector.tensor_copy(picked_scales[:], scale_table[:].indirect(offsets[:]))
+        picked_words = [pool.tile([P, HS], U32, name="picked_words%d" % h, align_bytes=64) for h in range(HALVES)]
+        for h in range(HALVES):
+            cols = slice(h * HS // 16, (h + 1) * HS // 16)
+            nc.vector.tensor_copy(picked_words[h][:], word_table[:].bitcast(U32).indirect(offsets[:, cols]))
+
+        nc.scalar.copy(grouped_view(1), raw_view(1))
+        quantize(1)
+
+        y = {}
+        for i in range(2):
+            for h in range(HALVES):
+                y[i, h] = psum.tile([P, HS], F32, name="y%d%d" % (i, h))
+                nc.tensor.matmul_mx(
+                    out=y[i, h][:],
+                    lhsT=w_codes[i][:].bitcast(FP8X4),
+                    lhsT_scale=w_scales[i][:],
+                    rhs=picked_words[h][:].bitcast(FP8X4),
+                    rhs_scale=picked_scales[:, h * HS : (h + 1) * HS],
+                    start=True,
+                    stop=True,
+                )
+
+        e = {}
+        for h in range(HALVES):
+            for i in range(2):
+                dosed = pool.tile([P, D, HV], F32, name="dosed%d%d" % (i, h))
+                nc.vector.tensor_tensor(dosed[:], y[i, h][:].rearrange("p (v d) -> p d v", d=D), dose_rows[:, h], MULT)
+                pair_sum = pool.tile([P, HV], F32, name="pair_sum%d%d" % (i, h))
+                nc.vector.tensor_tensor(pair_sum[:], dosed[:, 0, :], dosed[:, 1, :], ADD)
+                e[i, h] = pool.tile([P, HV], F32, name="e%d%d" % (i, h))
+                nc.scalar.activation(e[i, h][:], pair_sum[:], EXP, bias=bias[i][:], scale=1.0 / D)
+
+        for h in range(HALVES):
+            unbound = pool.tile([P, HV], F32, name="unbound%d" % h)
+            nc.vector.scalar_tensor_tensor(unbound[:], e[0, h][:], 1.0, e[1, h][:], ADD, MULT)
+            denom = pool.tile([P, HV], F32, name="denom%d" % h)
+            inv_amp = inv_amp_bank[:, :, h * HV // 2 : (h + 1) * HV // 2].rearrange("p c w -> p w c")
+            nc.vector.scalar_tensor_tensor(denom[:].rearrange("p (w c) -> p w c", c=2), unbound[:].rearrange("p (w c) -> p w c", c=2), 1.0, inv_amp, ADD, MULT)
+            signal = pool.tile([P, HV], F32, name="signal%d" % h)
+            nc.vector.reciprocal(signal[:], denom[:])
+            nc.sync.dma_start(out[:, h * HV : (h + 1) * HV], signal[:])

@@ -35,22 +35,21 @@ def tile_picked_ythermo_bind_p_kernel(tc, x_words, x_scales, w1, w2, dose, gf0, 
         word_table = pool.tile([P, T], I32, name="word_table", align_bytes=64)
         w_raw = [pool.tile([P, PACK, N], F32, name="w_raw%d" % i, align_bytes=64) for i in range(2)]
 
+        dose_cols = pool.tile([P, 4], F32, name="dose_cols")
+        amp_cols = pool.tile([P, 2], F32, name="amp_cols")
+        bias = [pool.tile([P, 1], F32, name="bias%d" % i) for i in range(2)]
         nc.vector.memset(scale_table[:].bitcast(I32), 0)
         nc.sync.dma_start(w_raw[0][:], w1.rearrange("(p j) n -> p j n", j=PACK))
         nc.sync.dma_start(offsets[:], offs)
         for q in range(4):
             nc.sync.dma_start(scale_table[32 * q : 32 * q + 4, :].bitcast(I32), x_scales[0, 4 * q : 4 * q + 4, :].bitcast(I32))
+        nc.sync.dma_start(dose_cols[:], dose[0].rearrange("(p c) -> p c", c=4))
         nc.sync.dma_start(word_table[:], x_words[0].rearrange("p n t -> p (n t)").bitcast(I32))
         nc.sync.dma_start(w_raw[1][:], w2.rearrange("(p j) n -> p j n", j=PACK))
-
-        bias = [pool.tile([P, 1], F32, name="bias%d" % i) for i in range(2)]
+        nc.sync.dma_start(amp_cols[:], amp[0].rearrange("(p c) -> p c", c=2))
         nc.sync.dma_start(bias[0][:], gf0)
         nc.sync.dma_start(bias[1][:], gb0)
 
-        dose_cols = pool.tile([P, 4], F32, name="dose_cols")
-        amp_cols = pool.tile([P, 2], F32, name="amp_cols")
-        nc.gpsimd.dma_start(dose_cols[:], dose[0].rearrange("(p c) -> p c", c=4))
-        nc.gpsimd.dma_start(amp_cols[:], amp[0].rearrange("(p c) -> p c", c=2))
         identity = pool.tile([P, P], F32, name="identity")
         make_identity(nc, identity[:])
 
@@ -108,22 +107,49 @@ def tile_picked_ythermo_bind_p_kernel(tc, x_words, x_scales, w1, w2, dose, gf0, 
                     stop=True,
                 )
 
-        e = {}
-        for h in range(HALVES):
-            for i in range(2):
-                dosed = pool.tile([P, D, HV], F32, name="dosed%d%d" % (i, h))
-                nc.vector.tensor_tensor(dosed[:], y[i, h][:].rearrange("p (v d) -> p d v", d=D), dose_rows[:, h], MULT)
-                pair_sum = pool.tile([P, HV], F32, name="pair_sum%d%d" % (i, h))
-                nc.vector.tensor_tensor(pair_sum[:], dosed[:, 0, :], dosed[:, 1, :], ADD)
-                e[i, h] = pool.tile([P, HV], F32, name="e%d%d" % (i, h))
-                nc.scalar.activation(e[i, h][:], pair_sum[:], EXP, bias=bias[i][:], scale=1.0 / D)
+        dosed, e, unbound, denom = {}, {}, {}, {}
+        signal = [pool.tile([P, HV], F32, name="signal%d" % h) for h in range(HALVES)]
 
-        for h in range(HALVES):
-            unbound = pool.tile([P, HV], F32, name="unbound%d" % h)
-            nc.vector.scalar_tensor_tensor(unbound[:], e[0, h][:], 1.0, e[1, h][:], ADD, MULT)
-            denom = pool.tile([P, HV], F32, name="denom%d" % h)
+        def weigh(i, h):
+            dosed[i, h] = pool.tile([P, D, HV], F32, name="dosed%d%d" % (i, h))
+            nc.vector.tensor_tensor(dosed[i, h][:], y[i, h][:].rearrange("p (v d) -> p d v", d=D), dose_rows[:, h], MULT)
+
+        def add_and_exp(i, h):
+            pair_sum = pool.tile([P, HV], F32, name="pair_sum%d%d" % (i, h))
+            nc.vector.tensor_tensor(pair_sum[:], dosed[i, h][:, 0, :], dosed[i, h][:, 1, :], ADD)
+            e[i, h] = pool.tile([P, HV], F32, name="e%d%d" % (i, h))
+            nc.scalar.activation(e[i, h][:], pair_sum[:], EXP, bias=bias[i][:], scale=1.0 / D)
+
+        def make_unbound(h):
+            unbound[h] = pool.tile([P, HV], F32, name="unbound%d" % h)
+            nc.vector.scalar_tensor_tensor(unbound[h][:], e[0, h][:], 1.0, e[1, h][:], ADD, MULT)
+
+        def make_denom(h):
+            denom[h] = pool.tile([P, HV], F32, name="denom%d" % h)
             inv_amp = inv_amp_bank[:, :, h * HV // 2 : (h + 1) * HV // 2].rearrange("p c w -> p w c")
-            nc.vector.scalar_tensor_tensor(denom[:].rearrange("p (w c) -> p w c", c=2), unbound[:].rearrange("p (w c) -> p w c", c=2), 1.0, inv_amp, ADD, MULT)
-            signal = pool.tile([P, HV], F32, name="signal%d" % h)
-            nc.vector.reciprocal(signal[:], denom[:])
-            nc.sync.dma_start(out[:, h * HV : (h + 1) * HV], signal[:])
+            nc.vector.scalar_tensor_tensor(denom[h][:].rearrange("p (w c) -> p w c", c=2), unbound[h][:].rearrange("p (w c) -> p w c", c=2), 1.0, inv_amp, ADD, MULT)
+
+        def invert(h, lo, hi):
+            nc.vector.reciprocal(signal[h][:, lo:hi], denom[h][:, lo:hi])
+
+        def store(h):
+            nc.sync.dma_start(out[:, h * HV : (h + 1) * HV], signal[h][:])
+
+        weigh(0, 0)
+        weigh(0, 1)
+        add_and_exp(0, 0)
+        weigh(1, 0)
+        add_and_exp(0, 1)
+        add_and_exp(1, 0)
+        weigh(1, 1)
+        make_unbound(0)
+        add_and_exp(1, 1)
+        make_denom(0)
+        invert(0, 0, 48)
+        make_unbound(1)
+        invert(0, 48, 88)
+        make_denom(1)
+        invert(0, 88, 128)
+        store(0)
+        invert(1, 0, 128)
+        store(1)

@@ -35,7 +35,7 @@ def tile_picked_ythermo_bind_p_kernel(tc, x_words, x_scales, w1, w2, dose, gf0, 
         word_table = pool.tile([P, T], I32, name="word_table", align_bytes=64)
         w_raw = [pool.tile([P, PACK, N], F32, name="w_raw%d" % i, align_bytes=64) for i in range(2)]
 
-        dose_cols = pool.tile([P, 4], F32, name="dose_cols")
+        dose_cols = pool.tile([P, 4], F32, name="dose_cols", tag="late_stage", align_bytes=64)
         amp_cols = pool.tile([P, 2], F32, name="amp_cols")
         bias = [pool.tile([P, 1], F32, name="bias%d" % i) for i in range(2)]
         nc.vector.memset(scale_table[:].bitcast(I32), 0)
@@ -56,11 +56,8 @@ def tile_picked_ythermo_bind_p_kernel(tc, x_words, x_scales, w1, w2, dose, gf0, 
         inv_amp_cols = pool.tile([P, 2], F32, name="inv_amp_cols")
         nc.vector.reciprocal(inv_amp_cols[:], amp_cols[:])
         dose_bank = psum.tile([P, 4, P], F32, name="dose_bank")
-        inv_amp_bank = psum.tile([P, 2, P], F32, name="inv_amp_bank")
         for c in range(4):
             nc.tensor.transpose(dose_bank[:, c, :], dose_cols[:, c : c + 1].to_broadcast([P, P]), identity[:])
-        for c in range(2):
-            nc.tensor.transpose(inv_amp_bank[:, c, :], inv_amp_cols[:, c : c + 1].to_broadcast([P, P]), identity[:])
         dose_rows = pool.tile([P, HALVES, D, HV], F32, name="dose_rows")
         nc.scalar.copy(
             dose_rows[:].rearrange("q h d (w e) -> q h d w e", e=2),
@@ -69,7 +66,7 @@ def tile_picked_ythermo_bind_p_kernel(tc, x_words, x_scales, w1, w2, dose, gf0, 
 
         w_codes = [pool.tile([P, N], U32, name="w_codes%d" % i, align_bytes=64) for i in range(2)]
         w_scales = [pool.tile([P, N], U8, name="w_scales%d" % i, align_bytes=64) for i in range(2)]
-        w_grouped = [pool.tile([P, N, PACK], BF16, name="w_grouped%d" % i, align_bytes=64) for i in range(2)]
+        w_grouped = [pool.tile([P, N, PACK], BF16, name="w_grouped%d" % i, tag=("early_stage", "late_stage")[i], align_bytes=64) for i in range(2)]
 
         def grouped_view(i):
             return w_grouped[i][:].rearrange("p (c e) j -> p c j e", e=4)
@@ -93,12 +90,13 @@ def tile_picked_ythermo_bind_p_kernel(tc, x_words, x_scales, w1, w2, dose, gf0, 
         nc.scalar.copy(grouped_view(1), raw_view(1))
         quantize(1)
 
-        y = {}
+        y, bank = {}, {}
         for i in range(2):
             for h in range(HALVES):
-                y[i, h] = psum.tile([P, HS], F32, name="y%d%d" % (i, h))
+                bank[i, h] = psum.tile([P, 2, HS], F32, name="bank%d%d" % (i, h))
+                y[i, h] = bank[i, h][:, 0, :]
                 nc.tensor.matmul_mx(
-                    out=y[i, h][:],
+                    out=y[i, h],
                     lhsT=w_codes[i][:].bitcast(FP8X4),
                     lhsT_scale=w_scales[i][:],
                     rhs=picked_words[h][:].bitcast(FP8X4),
@@ -110,13 +108,15 @@ def tile_picked_ythermo_bind_p_kernel(tc, x_words, x_scales, w1, w2, dose, gf0, 
         dosed, e, unbound, denom = {}, {}, {}, {}
         signal = [pool.tile([P, HV], F32, name="signal%d" % h) for h in range(HALVES)]
 
+        dosed_all = [pool.tile([P, HALVES, D, HV], F32, name="dosed%d" % i, tag=("late_stage", "dosed")[i], align_bytes=64) for i in range(2)]
+
         def weigh(i, h):
-            dosed[i, h] = pool.tile([P, D, HV], F32, name="dosed%d%d" % (i, h))
-            nc.vector.tensor_tensor(dosed[i, h][:], y[i, h][:].rearrange("p (v d) -> p d v", d=D), dose_rows[:, h], MULT)
+            dosed[i, h] = dosed_all[i][:, h]
+            nc.vector.tensor_tensor(dosed[i, h], y[i, h].rearrange("p (v d) -> p d v", d=D), dose_rows[:, h], MULT)
 
         def add_and_exp(i, h):
             pair_sum = pool.tile([P, HV], F32, name="pair_sum%d%d" % (i, h))
-            nc.vector.tensor_tensor(pair_sum[:], dosed[i, h][:, 0, :], dosed[i, h][:, 1, :], ADD)
+            (nc.gpsimd if i == 0 else nc.vector).tensor_tensor(pair_sum[:], dosed[i, h][:, 0, :], dosed[i, h][:, 1, :], ADD)
             e[i, h] = pool.tile([P, HV], F32, name="e%d%d" % (i, h))
             nc.scalar.activation(e[i, h][:], pair_sum[:], EXP, bias=bias[i][:], scale=1.0 / D)
 
@@ -138,18 +138,19 @@ def tile_picked_ythermo_bind_p_kernel(tc, x_words, x_scales, w1, w2, dose, gf0, 
         weigh(0, 0)
         weigh(0, 1)
         add_and_exp(0, 0)
-        weigh(1, 0)
         add_and_exp(0, 1)
-        add_and_exp(1, 0)
+        weigh(1, 0)
         weigh(1, 1)
-        make_unbound(0)
+        inv_amp_bank = bank[1, 1][:, 1, :].rearrange("p (c w) -> p c w", c=2)
+        for c in range(2):
+            nc.tensor.transpose(inv_amp_bank[:, c, :], inv_amp_cols[:, c : c + 1].to_broadcast([P, P]), identity[:])
+        add_and_exp(1, 0)
         add_and_exp(1, 1)
-        make_denom(0)
-        invert(0, 0, 48)
+        make_unbound(0)
         make_unbound(1)
-        invert(0, 48, 88)
+        make_denom(0)
         make_denom(1)
-        invert(0, 88, 128)
+        invert(0, 0, 128)
         store(0)
         invert(1, 0, 128)
         store(1)

from contextlib import ExitStack

import concourse.mybir as mybir
from concourse.masks import make_identity

K, T, S, D, N, V = 512, 2048, 512, 2, 128, 256
FLOPS = 2 * 2 * K * N * S

F32 = mybir.dt.float32
BF16 = mybir.dt.bfloat16
I32 = mybir.dt.int32
U32 = mybir.dt.uint32
U16 = mybir.dt.uint16
U8 = mybir.dt.uint8
FP8X4 = mybir.dt.float8_e4m3fn_x4
ADD = mybir.AluOpType.add
MULT = mybir.AluOpType.mult
EXP = mybir.ActivationFunctionType.Exp

P = 128
PACK = 4
HALVES = 2
HS = S // HALVES
HV = V // HALVES


def tile_picked_ythermo_bind_p_kernel(tc, x_words, x_scales, w1, w2, dose, gf0, gb0, amp, offs, out):
    nc = tc.nc
    with ExitStack() as ctx:
        pool = ctx.enter_context(tc.tile_pool(name="pool", bufs=1))
        psum = ctx.enter_context(tc.psum_pool(name="psum", bufs=1))

        offsets = pool.tile([P, S // 16], U16, name="offsets")
        scale_table = pool.tile([P, T], U8, name="scale_table", align_bytes=64)
        word_table = pool.tile([P, T], I32, name="word_table", align_bytes=64)
        w_raw = [pool.tile([P, PACK, N], F32, name="w_raw%d" % i, align_bytes=64) for i in range(2)]

        dose_cols = pool.tile([P, 4], F32, name="dose_cols", tag="late_stage", align_bytes=64)
        amp_cols = pool.tile([P, 2], F32, name="amp_cols")
        bias = [pool.tile([P, 1], F32, name="bias%d" % i) for i in range(2)]
        nc.vector.memset(scale_table[:].bitcast(I32), 0)
        nc.sync.dma_start(w_raw[0][:], w1.rearrange("(p j) n -> p j n", j=PACK))
        nc.sync.dma_start(offsets[:], offs)
        for q in range(4):
            nc.sync.dma_start(scale_table[32 * q : 32 * q + 4, :].bitcast(I32), x_scales[0, 4 * q : 4 * q + 4, :].bitcast(I32))
        nc.sync.dma_start(dose_cols[:], dose[0].rearrange("(p c) -> p c", c=4))
        nc.sync.dma_start(word_table[:], x_words[0].rearrange("p n t -> p (n t)").bitcast(I32))
        nc.sync.dma_start(w_raw[1][:], w2.rearrange("(p j) n -> p j n", j=PACK))
        nc.sync.dma_start(amp_cols[:], amp[0].rearrange("(p c) -> p c", c=2))
        nc.sync.dma_start(bias[0][:], gf0)
        nc.sync.dma_start(bias[1][:], gb0)

        identity = pool.tile([P, P], F32, name="identity")
        make_identity(nc, identity[:])

        inv_amp_cols = pool.tile([P, 2], F32, name="inv_amp_cols")
        nc.vector.reciprocal(inv_amp_cols[:], amp_cols[:])
        dose_bank = psum.tile([P, 4, P], F32, name="dose_bank")
        for c in range(4):
            nc.tensor.transpose(dose_bank[:, c, :], dose_cols[:, c : c + 1].to_broadcast([P, P]), identity[:])
        dose_rows = pool.tile([P, HALVES, D, HV], F32, name="dose_rows")
        nc.scalar.copy(
            dose_rows[:].rearrange("q h d (w e) -> q h d w e", e=2),
            dose_bank[:].rearrange("q (e d) (h w) -> q h d w e", d=D, h=HALVES),
        )

        w_codes = [pool.tile([P, N], U32, name="w_codes%d" % i, align_bytes=64) for i in range(2)]
        w_scales = [pool.tile([P, N], U8, name="w_scales%d" % i, align_bytes=64) for i in range(2)]
        w_grouped = [pool.tile([P, N, PACK], BF16, name="w_grouped%d" % i, tag=("early_stage", "late_stage")[i], align_bytes=64) for i in range(2)]

        def grouped_view(i):
            return w_grouped[i][:].rearrange("p (c e) j -> p c j e", e=4)

        def raw_view(i):
            return w_raw[i][:].rearrange("p j (c e) -> p c j e", e=4)

        def quantize(i):
            nc.vector.quantize_mx(out=w_codes[i][:].bitcast(FP8X4), scales=w_scales[i][:], in_=w_grouped[i][:].rearrange("p n j -> p (n j)"))

        nc.vector.tensor_copy(grouped_view(0), raw_view(0))
        quantize(0)

        picked_scales = pool.tile([P, S], U8, name="picked_scales", align_bytes=64)
        nc.vector.tensor_copy(picked_scales[:], scale_table[:].indirect(offsets[:]))
        picked_words = [pool.tile([P, HS], U32, name="picked_words%d" % h, align_bytes=64) for h in range(HALVES)]
        for h in range(HALVES):
            cols = slice(h * HS // 16, (h + 1) * HS // 16)
            nc.vector.tensor_copy(picked_words[h][:], word_table[:].bitcast(U32).indirect(offsets[:, cols]))

        nc.scalar.copy(grouped_view(1), raw_view(1))
        quantize(1)

        y, bank = {}, {}
        for i in range(2):
            for h in range(HALVES):
                bank[i, h] = psum.tile([P, 2, HS], F32, name="bank%d%d" % (i, h))
                y[i, h] = bank[i, h][:, 0, :]
                nc.tensor.matmul_mx(
                    out=y[i, h],
                    lhsT=w_codes[i][:].bitcast(FP8X4),
                    lhsT_scale=w_scales[i][:],
                    rhs=picked_words[h][:].bitcast(FP8X4),
                    rhs_scale=picked_scales[:, h * HS : (h + 1) * HS],
                    start=True,
                    stop=True,
                )

        dosed, e, unbound, denom = {}, {}, {}, {}
        signal = [pool.tile([P, HV], F32, name="signal%d" % h) for h in range(HALVES)]

        dosed_all = [pool.tile([P, HALVES, D, HV], F32, name="dosed%d" % i, tag=("late_stage", "dosed")[i], align_bytes=64) for i in range(2)]

        def weigh(i, h):
            dosed[i, h] = dosed_all[i][:, h]
            nc.vector.tensor_tensor(dosed[i, h], y[i, h].rearrange("p (v d) -> p d v", d=D), dose_rows[:, h], MULT)

        def add_and_exp(i, h):
            pair_sum = pool.tile([P, HV], F32, name="pair_sum%d%d" % (i, h))
            (nc.gpsimd if i == 0 else nc.vector).tensor_tensor(pair_sum[:], dosed[i, h][:, 0, :], dosed[i, h][:, 1, :], ADD)
            e[i, h] = pool.tile([P, HV], F32, name="e%d%d" % (i, h))
            nc.scalar.activation(e[i, h][:], pair_sum[:], EXP, bias=bias[i][:], scale=1.0 / D)

        def make_unbound(h):
            unbound[h] = pool.tile([P, HV], F32, name="unbound%d" % h)
            nc.vector.scalar_tensor_tensor(unbound[h][:], e[0, h][:], 1.0, e[1, h][:], ADD, MULT)

        def make_denom(h):
            denom[h] = pool.tile([P, HV], F32, name="denom%d" % h)
            inv_amp = inv_amp_bank[:, :, h * HV // 2 : (h + 1) * HV // 2].rearrange("p c w -> p w c")
            nc.vector.scalar_tensor_tensor(denom[h][:].rearrange("p (w c) -> p w c", c=2), unbound[h][:].rearrange("p (w c) -> p w c", c=2), 1.0, inv_amp, ADD, MULT)

        def invert(h, lo, hi):
            nc.vector.reciprocal(signal[h][:, lo:hi], denom[h][:, lo:hi])

        def store(h):
            nc.sync.dma_start(out[:, h * HV : (h + 1) * HV], signal[h][:])

        weigh(0, 0)
        weigh(0, 1)
        add_and_exp(0, 0)
        add_and_exp(0, 1)
        weigh(1, 0)
        weigh(1, 1)
        inv_amp_bank = bank[1, 1][:, 1, :].rearrange("p (c w) -> p c w", c=2)
        for c in range(2):
            nc.tensor.transpose(inv_amp_bank[:, c, :], inv_amp_cols[:, c : c + 1].to_broadcast([P, P]), identity[:])
        add_and_exp(1, 0)
        add_and_exp(1, 1)
        make_unbound(0)
        make_unbound(1)
        make_denom(0)
        make_denom(1)
        invert(0, 0, 128)
        store(0)
        invert(1, 0, 128)
        store(1)
